import numpy as np, ml_dtypes
CORES = [76,84,92,100,108,116,124]
N = 7
TK = 128
def setup_inputs(rng):
    return {"b": rng.standard_normal((N, 128, TK), dtype=np.float32).astype(ml_dtypes.bfloat16), "l": (rng.standard_normal((N, 128, N * 128), dtype=np.float32) / 16).astype(ml_dtypes.bfloat16)}
def setup_inputs_big(rng):
    d = setup_inputs(rng)
    for k in ("b",): d[k] = (d[k].astype(np.float32) * 1048576.0).astype(d[k].dtype)
    return d
def setup_inputs_small(rng):
    d = setup_inputs(rng)
    for k in ("b",): d[k] = (d[k].astype(np.float32) * (1 / 1048576.0)).astype(d[k].dtype)
    return d
def setup_inputs_apart(rng):
    d = setup_inputs(rng)
    f = (10.0 ** rng.permutation(np.linspace(-1.5, 1.5, N))).astype(np.float32).reshape(N, 1, 1)
    for k in ("b",): d[k] = (d[k].astype(np.float32) * f).astype(d[k].dtype)
    return d
def reference(b, l):
    B, L = b.astype(np.float64), l.astype(np.float64)
    y = np.zeros((N, 128, TK))
    for r in range(N):
        acc = B[r].copy()
        for s in range(r):
            acc -= L[r][:, 128 * s:128 * s + 128].T @ y[s]
        y[r] = acc
    return {"y": y.astype(ml_dtypes.bfloat16)}

from concourse.bass import DstId, RemoteDMATransfer
from concourse.mybir import AluOpType

N = 7
U = 128
PIECES = (1, 2, 1, 2, 2, 2)
N1 = 8
N2 = 8
NB = 8
CAP = 3


def _w(s):
    return (s + 1) * U


def _off(s):
    return U * (s * (s + 1) // 2)


SCRATCH = {
    "rows": ("sbuf", [128, _off(N)], "bfloat16"),
    "ys": ("sbuf", [128, N * U], "bfloat16"),
}
for _s in range(N - 1):
    SCRATCH["d%d" % _s] = ("dram", [PIECES[_s], 128, _w(_s) // PIECES[_s]], "bfloat16")
for _k in range(1, N):
    SCRATCH["p%d" % _k] = ("psum", [128, 512], "float32")

SEMAPHORES = (["ld", "own", "sa", "sb", "rin", "st"] + ["a%d" % s for s in range(N - 1)]
              + ["m%d" % k for k in range(1, N)] + ["v%d" % k for k in range(1, N)])


def _bits(mask):
    return [e for e in range(mask.bit_length()) if (mask >> e) & 1]


def _mk(engs):
    m = 0
    for e in engs:
        m |= 1 << e
    return m


def _plan(cores, topo, s):
    src = cores[s]
    later = list(range(N - 1, s, -1))
    direct = [q for q in later if topo.may_write(src, cores[q])]
    far = [q for q in later if not topo.may_write(src, cores[q])]
    cand = [c for c in range(topo.CHIPS * topo.CORES_PER_CHIP)
            if topo.chip(c) == topo.chip(src) and c not in cores
            and all(topo.may_write(c, cores[q]) for q in far)]
    near = [c for c in cand if topo.die(c) == topo.die(src)]
    away = [c for c in cand if topo.die(c) != topo.die(src)]
    order = []
    for i in range(max(len(near), len(away))):
        order += near[i:i + 1] + away[i:i + 1]
    P = PIECES[s]
    if len(far) * P <= len(order):
        groups = [[(p, q)] for q in far for p in range(P)]
    else:
        groups = [[(p, far[0])] for p in range(P)] + [[(p, q) for p in range(P)] for q in far[1:]]
    return direct, list(zip(order, groups))


def _arrive(cores, topo, s, q):
    direct, jobs = _plan(cores, topo, s)
    if q in direct:
        return NB
    return sum(N2 // len(grp) for _, grp in jobs for (_, qq) in grp if qq == q)


def _dst(topo, c):
    rid, pid, _ = topo.addr(c)
    return DstId(rid=rid, pnc=pid)


def _piece_cols(s, p):
    w = _w(s) // PIECES[s]
    return _off(s) + p * w, _off(s) + (p + 1) * w


def _send_row(g, core, T, topo, s):
    cores = list(T.cores)
    direct, jobs = _plan(cores, topo, s)
    P = PIECES[s]
    w = _w(s) // P
    d = T["d%d" % s]
    loads = []
    for p in range(P):
        c0, c1 = p * w, (p + 1) * w
        if c0 < U:
            loads.append((d[p, :, 0:U], T.b[:, :]))
        lo = max(c0, U)
        if lo < c1:
            loads.append((d[p, :, lo - c0:w], T.l[:, lo - U:c1 - U]))
    qs = [g.sync, g.scalar]
    for i, (o, a) in enumerate(loads):
        qs[i % 2].dma_start(o, a).then_inc(T.sem.ld, 16)
    g.wait_ge(T.sem.ld, 16 * len(loads))

    off_mask = _mk(range(64))
    for q in range(s + 1, N):
        off_mask &= topo.mask(core, cores[q])
    on_mask = _mk(range(64))
    for c, _ in jobs:
        on_mask &= topo.mask(core, c)
    off_e = _bits(off_mask)
    on_e = [e for e in _bits(on_mask) if e not in off_e] + [e for e in _bits(on_mask) if e in off_e]
    na = N1 // P
    tr = []
    for p in range(P):
        to = [c for c, grp in jobs if any(pp == p for pp, _ in grp)]
        tr.append(RemoteDMATransfer(dst_ids=[_dst(topo, c) for c in to], dma_engine_mask=_mk(on_e[p * na:(p + 1) * na]),
                                    remote_sem=T.sem.rin, srcs=[d[p]], dsts=[d[p] for _ in to], alu_op=0))
    g.remote_dma_fused(tr, local_sem=T.sem.sa)
    if direct:
        nb = NB // P
        tr = []
        for p in range(P):
            a, b = _piece_cols(s, p)
            tr.append(RemoteDMATransfer(dst_ids=[_dst(topo, cores[q]) for q in direct],
                                        dma_engine_mask=_mk(off_e[p * nb:(p + 1) * nb]), remote_sem=T.sem["a%d" % s],
                                        srcs=[d[p]], dsts=[T.rows[:, a:b] for _ in direct], alu_op=0))
        g.remote_dma_fused(tr, local_sem=T.sem.sb)
    g.wait_ge(T.sem.sa, N1)
    if direct:
        g.wait_ge(T.sem.sb, NB)


def _forward(g, core, T, topo, s, grp):
    cores = list(T.cores)
    d = T["d%d" % s]
    g.wait_ge(T.sem.rin, (N1 // PIECES[s]) * len(set(p for p, _ in grp)))
    n = N2 // len(grp)
    tr = []
    for i, (p, q) in enumerate(grp):
        a, b = _piece_cols(s, p)
        engs = _bits(topo.mask(core, cores[q]))
        tr.append(RemoteDMATransfer(dst_ids=[_dst(topo, cores[q])], dma_engine_mask=_mk(engs[i * n:(i + 1) * n]),
                                    remote_sem=T.sem["a%d" % s], srcs=[d[p]], dsts=[T.rows[:, a:b]], alu_op=0))
    g.remote_dma_fused(tr, local_sem=T.sem.sa)
    g.wait_ge(T.sem.sa, n * len(grp))


def _order(cores, topo, r):
    def early(j):
        return topo.may_write(cores[j], cores[r]) if j < r else r == N - 1
    out = []
    if early(0):
        out = [(j, 0) for j in range(2, r + 1) if early(j) and (j <= 2 or j == r)]
    pending = [(j, s) for j in range(2, r + 1) for s in range(j - 1) if (j, s) not in out]
    for k in range(1, r + 1):
        out.append((k, k - 1))
        avail = [x for x in pending if x[1] <= k - 1]
        must = [x for x in avail if x[0] == k + 1]
        rest = [x for x in avail if x[0] != k + 1 and (early(x[0]) or x[0] <= k + 2)]
        rest.sort(key=lambda x: (not early(x[0]), x[0], x[1]))
        take = must + rest[:max(0, CAP - len(must))]
        take.sort(key=lambda x: (not early(x[0]), x[0], x[1]))
        out += take
        pending = [x for x in pending if x not in take]
    return out


def _solve(g, core, T, topo, r):
    cores = list(T.cores)
    for q in (g.sync, g.scalar):
        if r < N - 1:
            q.wait_ge(T.sem.sa, N1)
    o = _off(r)
    g.sync.dma_start(T.rows[:, o + U:o + _w(r)], T.l[:, 0:U * r]).then_inc(T.sem.own, 16)
    g.scalar.dma_start(T.rows[:, o:o + U], T.b[:, :]).then_inc(T.sem.own, 16)

    def wait_row(q, j):
        if j == r:
            q.wait_ge(T.sem.own, 32)
        else:
            q.wait_ge(T.sem["a%d" % j], _arrive(cores, topo, j, r))

    def y(s):
        return T.rows[:, 0:U] if s == 0 else T.ys[:, s * U:(s + 1) * U]

    seen_rows, seen_y, done = set(), set(), {}
    for (k, s) in _order(cores, topo, r):
        for j in ((k, 0) if s == 0 else (k,)):
            if j not in seen_rows:
                seen_rows.add(j)
                wait_row(g.tensor, j)
        if s > 0 and s not in seen_y:
            seen_y.add(s)
            g.tensor.wait_ge(T.sem["v%d" % s], 1)
        done[k] = done.get(k, 0) + 1
        a = _off(k) + U * (s + 1)
        g.tensor.matmul(T["p%d" % k][:, 0:U], T.rows[:, a:a + U], y(s), start=done[k] == 1,
                        stop=done[k] == k).then_inc(T.sem["m%d" % k], 1)
    for k in range(1, r + 1):
        wait_row(g.vector, k)
        g.vector.wait_ge(T.sem["m%d" % k], k)
        g.vector.tensor_tensor(T.ys[:, k * U:(k + 1) * U], T.rows[:, _off(k):_off(k) + U], T["p%d" % k][:, 0:U],
                               AluOpType.subtract).then_inc(T.sem["v%d" % k], 1)
    g.sync.wait_ge(T.sem["v%d" % r], 1)
    g.sync.dma_start(T.y[:, :], T.ys[:, r * U:(r + 1) * U]).then_inc(T.sem.st, 16)
    g.sync.wait_ge(T.sem.st, 16)


def rank_program(g, core, T, topo):
    cores = list(T.cores)
    r = T.rank_of(core)
    if r is None:
        for s in range(N - 1):
            for c, grp in _plan(cores, topo, s)[1]:
                if c == core:
                    _forward(g, core, T, topo, s, grp)
        return
    if r < N - 1:
        _send_row(g, core, T, topo, r)
    if r == 0:
        g.scalar.dma_start(T.y[:, :], T.b[:, :]).then_inc(T.sem.st, 16)
        g.scalar.wait_ge(T.sem.st, 16)
    else:
        _solve(g, core, T, topo, r)
